import numpy as np
import ml_dtypes


def mxq(x, axis, fmt="e4m3"):
    dtype, down = {"e4m3": (ml_dtypes.float8_e4m3fn, 7), "e5m2": (ml_dtypes.float8_e5m2, 14)}[fmt]
    v = np.moveaxis(np.asarray(x, np.float32).astype(ml_dtypes.bfloat16).astype(np.float64), axis, -1)
    blocks = v.reshape(v.shape[:-1] + (-1, 32))
    amax = np.abs(blocks).max(-1, keepdims=True)
    byte = np.maximum(np.where(amax > 0, np.frexp(amax)[1] - 1 + 127, 0) - down, 1)
    scale = np.exp2(byte - 127.0)
    codes = (blocks / scale).astype(np.float32).astype(dtype).astype(np.float64)
    return np.moveaxis((codes * scale).reshape(v.shape), -1, axis)


WIDE = False


def mx_kscale(k):
    if not WIDE:
        return np.ones(k)
    levels = np.array([10, -10, 5, -5, 0])
    if k % 512:
        return np.exp2(np.random.permutation(np.resize(levels, k // 32))).repeat(32)
    a = np.empty((k // 512, 16))
    for p in range(k // 512):
        a[p, :8] = np.random.permutation(np.resize(levels, 8))
        for g in range(8):
            far = levels[np.abs(levels - a[p, g]) >= 10]
            a[p, g + 8] = far[np.random.randint(len(far))]
    return np.exp2(a.ravel()).repeat(32)


def f64(x):
    return np.asarray(x).astype(np.float64)


def striped(idx):
    return np.tile(idx.reshape(-1, 16).T, (8, 1)).astype(np.uint16)


def unstriped(offs):
    return offs[:16].T.reshape(-1).astype(np.int64)


def gelu(v):
    return 0.5 * v * (1.0 + np.tanh(np.sqrt(2.0 / np.pi) * (v + 0.044715 * v**3)))


K, T, E, C, N = 1024, 1280, 6, 128, 384


def by_expert(wq, xq):
    return np.concatenate([wq[e].T @ xq[:, e * C:(e + 1) * C] for e in range(E)], axis=1)


def setup_inputs():
    n = np.random.standard_normal
    s = mx_kscale(K)[:, None]
    return {
        "xT": (n((K, T)) * s).astype(np.float32),
        "w": (n((E, K, N)) / np.sqrt(K) / s[None]).astype(np.float32),
        "b": (0.3 * n((N, E))).astype(np.float32),
        "gate": np.tile(np.random.uniform(0.2, 1.0, E * C), (K, 1)).astype(np.float32),
        "offs": striped(np.random.permutation(T)[:E * C]),
    }


def reference(xT, w, b, gate, offs):
    idx = unstriped(offs)
    xq = mxq(f64(gate) * f64(xT)[:, idx], 0, "e4m3")
    y = by_expert(mxq(f64(w), 1, "e4m3"), xq)
    y = gelu(y + np.repeat(f64(b), C, axis=1))
    out = np.zeros((N, T))
    out[:, idx] = y
    return out

@@ -1,0 +1,206 @@
+from contextlib import ExitStack
+
+import concourse.mybir as mybir
+
+K, T, E, C, N = 1024, 1280, 6, 128, 384
+S = E * C
+FLOPS = 2 * K * N * S
+BYTES = 4 * (K * T + E * K * N + N * E + S + N * T) + 2 * S
+
+F32 = mybir.dt.float32
+BF16 = mybir.dt.bfloat16
+U32 = mybir.dt.uint32
+U16 = mybir.dt.uint16
+U8 = mybir.dt.uint8
+FP8X4 = mybir.dt.float8_e4m3fn_x4
+GELU = mybir.ActivationFunctionType.Gelu_apprx_tanh
+ADD = mybir.AluOpType.add
+MULT = mybir.AluOpType.mult
+
+P = 128
+PACK = 4
+PASSES = K // (P * PACK)
+ROW_TILES = N // P
+LIST_ROW = 16
+LOADS = "xxxxwxxwxxwwwwwwwwww"
+GROUPS = ((0, 1), (2, 3), (4, 5))
+XGROUPS = ((0, 256), (256, 768))
+X0GROUPS = ((0, 512), (512, 768))
+BY_PASS = 0
+LEAD = 0
+V_CASTS = ()
+V_IL = ()
+XFIRST = False
+HOLD = 2
+MERGE = False
+XLEAD = 2
+
+
+def tile_moe_pre_lin_gelu_kernel(tc, xT, w, b, gate, offs, out):
+    nc = tc.nc
+    with ExitStack() as ctx:
+        keep = ctx.enter_context(tc.tile_pool(name="keep", bufs=1))
+        stage = ctx.enter_context(tc.tile_pool(name="stage", bufs=4))
+        psum = ctx.enter_context(tc.psum_pool(name="psum", bufs=8))
+
+        offsets = keep.tile([P, S // LIST_ROW], U16, name="offsets")
+        nc.sync.dma_start(offsets[:], offs)
+        gate_all = keep.tile([P, S], F32, name="gate_all")
+        nc.sync.dma_start(gate_all[:], gate[0:P, :])
+        bias = keep.tile([P, ROW_TILES, E], F32, name="bias")
+
+        x_rows = xT.rearrange("(g p t) c -> g t p c", p=P, t=PACK)
+        w_rows = w.rearrange("e (g p j) n -> e g p j n", p=P, j=PACK)
+        x_raw = {}
+        w_raw = {}
+        x_pieces = [(g, t) for g in range(PASSES) for t in range(PACK)]
+        w_pieces = [(e, g) for e in range(E) for g in range(PASSES)]
+        nx = 0
+        nw = 0
+        for i, kind in enumerate(LOADS):
+            if kind == "x":
+                g, t = x_pieces[nx]
+                nx = nx + 1
+                x_raw[g, t] = keep.tile([P, T], F32, name="x_raw_%d_%d" % (g, t))
+                nc.sync.dma_start(x_raw[g, t][:], x_rows[g, t])
+            else:
+                e, g = w_pieces[nw]
+                nw = nw + 1
+                if g == 0:
+                    w_raw[e] = keep.tile([P, PASSES, PACK, N], F32, name="w_raw_%d" % e)
+                nc.sync.dma_start(w_raw[e][:, g], w_rows[e, g])
+            if i == 6:
+                nc.sync.dma_start(bias[:], b.rearrange("(r p) e -> p r e", p=P))
+
+        zeros = keep.tile([P, C], F32, name="zeros")
+        nc.gpsimd.memset(zeros[:], 0.0)
+        warm = keep.tile([P, 1], F32, name="warm")
+        nc.scalar.activation(warm[:], zeros[:, 0:1], GELU)
+
+        windows = []
+        for r in range(ROW_TILES):
+            windows.append(keep.tile([P, T], F32, name="window_%d" % r))
+            (nc.gpsimd if r == 2 else nc.vector).memset(windows[r][:], 0.0)
+        y = [keep.tile([P, S], F32, name="y_%d" % r) for r in range(ROW_TILES)]
+        x_codes = [keep.tile([P, S], U32, name="x_codes_%d" % g, align_bytes=64) for g in range(PASSES)]
+        x_scales = [keep.tile([P, S], U8, name="x_scales_%d" % g, align_bytes=64) for g in range(PASSES)]
+        w_codes = {}
+        w_scales = {}
+
+        def gather(dst, g, t, lo, hi):
+            src = x_raw[g, t][:].indirect(offsets[:, lo // LIST_ROW : hi // LIST_ROW])
+            nc.vector.tensor_tensor(dst, src, gate_all[:, lo:hi], MULT)
+
+        def quantize_x(src, g, lo, hi):
+            x_bf = stage.tile([P, (hi - lo) * PACK], BF16, name="x_bf", align_bytes=64)
+            (nc.vector.tensor_copy if (g, lo) in V_IL else nc.scalar.copy)(
+                x_bf[:].rearrange("p (c i j) -> p c j i", i=4, j=PACK),
+                src.rearrange("p j (c i) -> p c j i", i=4),
+            )
+            nc.vector.quantize_mx(out=x_codes[g][:, lo:hi].bitcast(FP8X4), scales=x_scales[g][:, lo:hi], in_=x_bf[:])
+
+        def quantize_w_pass(e, g):
+            w_bf = stage.tile([P, N * PACK], BF16, name="w_bf", align_bytes=64, bufs=6)
+            nc.scalar.copy(
+                w_bf[:].rearrange("p (c i j) -> p c j i", i=4, j=PACK),
+                w_raw[e][:, g].rearrange("p j (c i) -> p c j i", i=4),
+            )
+            codes = keep.tile([P, N], U32, name="wp_codes_%d_%d" % (e, g), align_bytes=64)
+            scales = keep.tile([P, N], U8, name="wp_scales_%d_%d" % (e, g), align_bytes=64)
+            for lo, hi in ((0, 2 * P), (2 * P, N)):
+                nc.vector.quantize_mx(
+                    out=codes[:, lo:hi].bitcast(FP8X4), scales=scales[:, lo:hi], in_=w_bf[:, lo * PACK : hi * PACK]
+                )
+            for r in range(ROW_TILES):
+                w_codes[e, r, g] = codes[:, r * P : (r + 1) * P]
+                w_scales[e, r, g] = scales[:, r * P : (r + 1) * P]
+
+        def quantize_w(e, r):
+            if (e, r, 0) in w_codes:
+                if (e, r, 1) not in w_codes:
+                    quantize_w_pass(e, 1)
+                return
+            w_bf = stage.tile([P, PASSES * P * PACK], BF16, name="w_bf", align_bytes=64, bufs=6)
+            (nc.vector.tensor_copy if (e, r) in V_CASTS else nc.scalar.copy)(
+                w_bf[:].rearrange("p (g c i j) -> p g c j i", g=PASSES, i=4, j=PACK),
+                w_raw[e][:, :, :, r * P : (r + 1) * P].rearrange("p g j (c i) -> p g c j i", i=4),
+            )
+            codes = keep.tile([P, PASSES * P], U32, name="w_codes_%d_%d" % (e, r), align_bytes=64)
+            scales = keep.tile([P, PASSES * P], U8, name="w_scales_%d_%d" % (e, r), align_bytes=64)
+            nc.vector.quantize_mx(out=codes[:].bitcast(FP8X4), scales=scales[:], in_=w_bf[:])
+            for g in range(PASSES):
+                w_codes[e, r, g] = codes[:, g * P : (g + 1) * P]
+                w_scales[e, r, g] = scales[:, g * P : (g + 1) * P]
+
+        def scatter(r, lo, hi):
+            window = windows[r][:].indirect(offsets[:, lo // LIST_ROW : hi // LIST_ROW])
+            if hi - lo >= T // 8:
+                nc.vector.tensor_copy(window, y[r][:, lo:hi])
+            else:
+                nc.vector.tensor_tensor(window, y[r][:, lo:hi], zeros[:, 0 : hi - lo], ADD)
+
+        def product(e, r):
+            slots = slice(e * C, (e + 1) * C)
+            acc = psum.tile([P, C], F32, name="acc")
+            for g in range(PASSES):
+                nc.tensor.matmul_mx(
+                    out=acc[:],
+                    lhsT=w_codes[e, r, g].bitcast(FP8X4),
+                    lhsT_scale=w_scales[e, r, g],
+                    rhs=x_codes[g][:, slots].bitcast(FP8X4),
+                    rhs_scale=x_scales[g][:, slots],
+                    start=(g == 0),
+                    stop=(g == PASSES - 1),
+                )
+            nc.scalar.activation(y[r][:, slots], acc[:], GELU, bias=bias[:, r, e : e + 1])
+
+        first = keep.tile([P, PACK, S], F32, name="gathered_0")
+        nx = 0
+        nw = 0
+        for kind in LOADS:
+            if nx == PASSES * PACK:
+                break
+            if kind == "w":
+                if nw < BY_PASS:
+                    quantize_w_pass(*w_pieces[nw])
+                nw = nw + 1
+                continue
+            g, t = x_pieces[nx]
+            nx = nx + 1
+            if g == 0:
+                gather(first[:, t, :], g, t, 0, S)
+                if t == PACK - 1:
+                    for lo, hi in X0GROUPS:
+                        quantize_x(first[:, :, lo:hi], g, lo, hi)
+
+        done = []
+
+        def x_group(lo, hi):
+            if lo in done:
+                return
+            done.append(lo)
+            part = keep.tile([P, PACK, hi - lo], F32, name="gathered_1", bufs=HOLD)
+            for t in range(PACK):
+                gather(part[:, t, :], 1, t, lo, hi)
+            quantize_x(part[:], 1, lo, hi)
+
+        if XFIRST:
+            for lo, hi in XGROUPS:
+                x_group(lo, hi)
+        steps = [(e, r) for group in GROUPS for r in range(ROW_TILES) for e in group]
+        ahead = 0
+        for i, (e, r) in enumerate(steps):
+            for lo, hi in XGROUPS:
+                if lo < (steps[min(i + XLEAD, len(steps) - 1)][0] + 1) * C:
+                    x_group(lo, hi)
+            while ahead < min(len(steps), i + 1 + LEAD):
+                quantize_w(*steps[ahead])
+                ahead = ahead + 1
+            product(e, r)
+            group = [q for q in GROUPS if e in q][0]
+            if not MERGE:
+                scatter(r, e * C, (e + 1) * C)
+            elif e == group[-1]:
+                scatter(r, group[0] * C, (e + 1) * C)
+            if e == E - 1:
+                nc.sync.dma_start(out[r * P : (r + 1) * P, :], windows[r][:])

@@ -22,25 +22,21 @@ PACK = 4
 PASSES = K // (P * PACK)
 ROW_TILES = N // P
 LIST_ROW = 16
-LOADS = "xxxxwxxwxxwwwwwwwwww"
-GROUPS = ((0, 1), (2, 3), (4, 5))
+LOADS = "xxxwxxxwxxwwwwwwwwww"
 XGROUPS = ((0, 256), (256, 768))
-X0GROUPS = ((0, 512), (512, 768))
-BY_PASS = 0
-LEAD = 0
-V_CASTS = ()
-V_IL = ()
-XFIRST = False
-HOLD = 2
-MERGE = False
-XLEAD = 2
+SPLIT_FROM = 7
+BY_ROWS = 5
+YLEAD = 1
+MERGE_FROM = 4
+V_COLS = (0, 384, 0, 0, 0, 0)
+HELD = (0, 2, 3, 4)
+BY_PASS = (0, 1, 2)
 
 
 def tile_moe_pre_lin_gelu_kernel(tc, xT, w, b, gate, offs, out):
     nc = tc.nc
     with ExitStack() as ctx:
         keep = ctx.enter_context(tc.tile_pool(name="keep", bufs=1))
-        stage = ctx.enter_context(tc.tile_pool(name="stage", bufs=4))
         psum = ctx.enter_context(tc.psum_pool(name="psum", bufs=8))
 
         offsets = keep.tile([P, S // LIST_ROW], U16, name="offsets")
@@ -81,126 +77,114 @@ def tile_moe_pre_lin_gelu_kernel(tc, xT, w, b, gate, offs, out):
         for r in range(ROW_TILES):
             windows.append(keep.tile([P, T], F32, name="window_%d" % r))
             (nc.gpsimd if r == 2 else nc.vector).memset(windows[r][:], 0.0)
-        y = [keep.tile([P, S], F32, name="y_%d" % r) for r in range(ROW_TILES)]
-        x_codes = [keep.tile([P, S], U32, name="x_codes_%d" % g, align_bytes=64) for g in range(PASSES)]
-        x_scales = [keep.tile([P, S], U8, name="x_scales_%d" % g, align_bytes=64) for g in range(PASSES)]
+        y_own = [keep.tile([P, max(1, E - MERGE_FROM) * C], F32, name="y_%d" % r) for r in range(ROW_TILES)]
+        x_codes = {}
+        x_scales = {}
         w_codes = {}
         w_scales = {}
+        gathered = [keep.tile([P, PACK, S], F32, name="gathered_%d" % g) for g in range(PASSES)]
 
-        def gather(dst, g, t, lo, hi):
+        def gather(g, t, lo, hi):
             src = x_raw[g, t][:].indirect(offsets[:, lo // LIST_ROW : hi // LIST_ROW])
-            nc.vector.tensor_tensor(dst, src, gate_all[:, lo:hi], MULT)
+            nc.vector.tensor_tensor(gathered[g][:, t, lo:hi], src, gate_all[:, lo:hi], MULT)
 
-        def quantize_x(src, g, lo, hi):
-            x_bf = stage.tile([P, (hi - lo) * PACK], BF16, name="x_bf", align_bytes=64)
-            (nc.vector.tensor_copy if (g, lo) in V_IL else nc.scalar.copy)(
-                x_bf[:].rearrange("p (c i j) -> p c j i", i=4, j=PACK),
-                src.rearrange("p j (c i) -> p c j i", i=4),
+        UNIT = PASSES * (C + N)
+        rounded = [keep.tile([P, UNIT * PACK], BF16, name="rounded_%d" % e, align_bytes=64) for e in range(E)]
+        codes = [keep.tile([P, UNIT], U32, name="codes_%d" % e, align_bytes=64) for e in range(E)]
+        scales = [keep.tile([P, UNIT], U8, name="scales_%d" % e, align_bytes=64) for e in range(E)]
+
+        def quantize(e, lo, hi):
+            nc.vector.quantize_mx(
+                out=codes[e][:, lo:hi].bitcast(FP8X4),
+                scales=scales[e][:, lo:hi],
+                in_=rounded[e][:, lo * PACK : hi * PACK],
             )
-            nc.vector.quantize_mx(out=x_codes[g][:, lo:hi].bitcast(FP8X4), scales=x_scales[g][:, lo:hi], in_=x_bf[:])
 
-        def quantize_w_pass(e, g):
-            w_bf = stage.tile([P, N * PACK], BF16, name="w_bf", align_bytes=64, bufs=6)
+        def round_x(g, e):
             nc.scalar.copy(
-                w_bf[:].rearrange("p (c i j) -> p c j i", i=4, j=PACK),
-                w_raw[e][:, g].rearrange("p j (c i) -> p c j i", i=4),
+                rounded[e][:, g * C * PACK : (g + 1) * C * PACK].rearrange("p (c i j) -> p c j i", i=4, j=PACK),
+                gathered[g][:, :, e * C : (e + 1) * C].rearrange("p j (c i) -> p c j i", i=4),
             )
-            codes = keep.tile([P, N], U32, name="wp_codes_%d_%d" % (e, g), align_bytes=64)
-            scales = keep.tile([P, N], U8, name="wp_scales_%d_%d" % (e, g), align_bytes=64)
-            for lo, hi in ((0, 2 * P), (2 * P, N)):
-                nc.vector.quantize_mx(
-                    out=codes[:, lo:hi].bitcast(FP8X4), scales=scales[:, lo:hi], in_=w_bf[:, lo * PACK : hi * PACK]
-                )
-            for r in range(ROW_TILES):
-                w_codes[e, r, g] = codes[:, r * P : (r + 1) * P]
-                w_scales[e, r, g] = scales[:, r * P : (r + 1) * P]
+            x_codes[e, g] = codes[e][:, g * C : (g + 1) * C]
+            x_scales[e, g] = scales[e][:, g * C : (g + 1) * C]
 
         def quantize_w(e, r):
-            if (e, r, 0) in w_codes:
-                if (e, r, 1) not in w_codes:
-                    quantize_w_pass(e, 1)
+            if e < BY_ROWS and r > 0:
                 return
-            w_bf = stage.tile([P, PASSES * P * PACK], BF16, name="w_bf", align_bytes=64, bufs=6)
-            (nc.vector.tensor_copy if (e, r) in V_CASTS else nc.scalar.copy)(
-                w_bf[:].rearrange("p (g c i j) -> p g c j i", g=PASSES, i=4, j=PACK),
-                w_raw[e][:, :, :, r * P : (r + 1) * P].rearrange("p g j (c i) -> p g c j i", i=4),
+            lo, n = (0, N) if e < BY_ROWS else (r * P, P)
+            base = PASSES * (C + lo)
+            dst = rounded[e][:, base * PACK : (base + PASSES * n) * PACK].rearrange(
+                "p (g c i j) -> p g c j i", g=PASSES, i=4, j=PACK
             )
-            codes = keep.tile([P, PASSES * P], U32, name="w_codes_%d_%d" % (e, r), align_bytes=64)
-            scales = keep.tile([P, PASSES * P], U8, name="w_scales_%d_%d" % (e, r), align_bytes=64)
-            nc.vector.quantize_mx(out=codes[:].bitcast(FP8X4), scales=scales[:], in_=w_bf[:])
-            for g in range(PASSES):
-                w_codes[e, r, g] = codes[:, g * P : (g + 1) * P]
-                w_scales[e, r, g] = scales[:, g * P : (g + 1) * P]
+            src = w_raw[e][:, :, :, lo : lo + n].rearrange("p g j (c i) -> p g c j i", i=4)
+            cut = V_COLS[e] * n // N // 4
+            if cut > 0:
+                nc.vector.tensor_copy(dst[:, :, 0:cut], src[:, :, 0:cut])
+            if cut < n // 4 and e in BY_PASS:
+                for g in range(PASSES):
+                    nc.scalar.copy(dst[:, g, cut : n // 4], src[:, g, cut : n // 4])
+            elif cut < n // 4:
+                nc.scalar.copy(dst[:, :, cut : n // 4], src[:, :, cut : n // 4])
+            quantize(e, base if lo > 0 else 0, base + PASSES * n)
+            for rr in range(lo // P, (lo + n) // P):
+                for g in range(PASSES):
+                    at = base + g * n + rr * P - lo
+                    w_codes[e, rr, g] = codes[e][:, at : at + P]
+                    w_scales[e, rr, g] = scales[e][:, at : at + P]
 
-        def scatter(r, lo, hi):
+        def y_place(e, r):
+            if e in HELD and e < MERGE_FROM and e + YLEAD < E:
+                return w_raw[e + YLEAD][:, 1, r, N - P : N]
+            if e < MERGE_FROM:
+                return gathered[0][:, r, e * C : (e + 1) * C]
+            return y_own[r][:, (e - MERGE_FROM) * C : (e - MERGE_FROM + 1) * C]
+
+        def scatter(r, lo, hi, src):
             window = windows[r][:].indirect(offsets[:, lo // LIST_ROW : hi // LIST_ROW])
             if hi - lo >= T // 8:
-                nc.vector.tensor_copy(window, y[r][:, lo:hi])
+                nc.vector.tensor_copy(window, src)
             else:
-                nc.vector.tensor_tensor(window, y[r][:, lo:hi], zeros[:, 0 : hi - lo], ADD)
+                nc.vector.tensor_tensor(window, src, zeros[:, 0 : hi - lo], ADD)
 
         def product(e, r):
-            slots = slice(e * C, (e + 1) * C)
             acc = psum.tile([P, C], F32, name="acc")
             for g in range(PASSES):
                 nc.tensor.matmul_mx(
                     out=acc[:],
                     lhsT=w_codes[e, r, g].bitcast(FP8X4),
                     lhsT_scale=w_scales[e, r, g],
-                    rhs=x_codes[g][:, slots].bitcast(FP8X4),
-                    rhs_scale=x_scales[g][:, slots],
+                    rhs=x_codes[e, g].bitcast(FP8X4),
+                    rhs_scale=x_scales[e, g],
                     start=(g == 0),
                     stop=(g == PASSES - 1),
                 )
-            nc.scalar.activation(y[r][:, slots], acc[:], GELU, bias=bias[:, r, e : e + 1])
+            nc.scalar.activation(y_place(e, r), acc[:], GELU, bias=bias[:, r, e : e + 1])
 
-        first = keep.tile([P, PACK, S], F32, name="gathered_0")
-        nx = 0
-        nw = 0
-        for kind in LOADS:
-            if nx == PASSES * PACK:
-                break
-            if kind == "w":
-                if nw < BY_PASS:
-                    quantize_w_pass(*w_pieces[nw])
-                nw = nw + 1
-                continue
-            g, t = x_pieces[nx]
-            nx = nx + 1
-            if g == 0:
-                gather(first[:, t, :], g, t, 0, S)
-                if t == PACK - 1:
-                    for lo, hi in X0GROUPS:
-                        quantize_x(first[:, :, lo:hi], g, lo, hi)
+        for i, (g, t) in enumerate(x_pieces):
+            for lo, hi in XGROUPS if i >= SPLIT_FROM else ((0, S),):
+                gather(g, t, lo, hi)
+            if t == PACK - 1:
+                for e in range(E):
+                    round_x(g, e)
 
-        done = []
-
-        def x_group(lo, hi):
-            if lo in done:
-                return
-            done.append(lo)
-            part = keep.tile([P, PACK, hi - lo], F32, name="gathered_1", bufs=HOLD)
-            for t in range(PACK):
-                gather(part[:, t, :], 1, t, lo, hi)
-            quantize_x(part[:], 1, lo, hi)
-
-        if XFIRST:
-            for lo, hi in XGROUPS:
-                x_group(lo, hi)
-        steps = [(e, r) for group in GROUPS for r in range(ROW_TILES) for e in group]
-        ahead = 0
-        for i, (e, r) in enumerate(steps):
-            for lo, hi in XGROUPS:
-                if lo < (steps[min(i + XLEAD, len(steps) - 1)][0] + 1) * C:
-                    x_group(lo, hi)
-            while ahead < min(len(steps), i + 1 + LEAD):
-                quantize_w(*steps[ahead])
-                ahead = ahead + 1
-            product(e, r)
-            group = [q for q in GROUPS if e in q][0]
-            if not MERGE:
-                scatter(r, e * C, (e + 1) * C)
-            elif e == group[-1]:
-                scatter(r, group[0] * C, (e + 1) * C)
-            if e == E - 1:
-                nc.sync.dma_start(out[r * P : (r + 1) * P, :], windows[r][:])
+        for r in range(ROW_TILES):
+            quantize_w(0, r)
+        for e in range(MERGE_FROM):
+            for r in range(ROW_TILES):
+                if e + 1 < E:
+                    quantize_w(e + 1, r)
+            for r in range(ROW_TILES):
+                product(e, r)
+                scatter(r, e * C, (e + 1) * C, y_place(e, r))
+                if e == E - 1:
+                    nc.sync.dma_start(out[r * P : (r + 1) * P, :], windows[r][:])
+        if MERGE_FROM < E:
+            for r in range(ROW_TILES + 1):
+                if r < ROW_TILES:
+                    for e in range(MERGE_FROM + 1, E):
+                        quantize_w(e, r)
+                if r > 0:
+                    for e in range(MERGE_FROM, E):
+                        product(e, r - 1)
+                    scatter(r - 1, MERGE_FROM * C, S, y_own[r - 1][:])
+                    nc.sync.dma_start(out[(r - 1) * P : r * P, :], windows[r - 1][:])

@@ -22,15 +22,13 @@ PACK = 4
 PASSES = K // (P * PACK)
 ROW_TILES = N // P
 LIST_ROW = 16
-LOADS = "xxxwxxxwxxwwwwwwwwww"
-XGROUPS = ((0, 256), (256, 768))
-SPLIT_FROM = 7
-BY_ROWS = 5
-YLEAD = 1
-MERGE_FROM = 4
-V_COLS = (0, 384, 0, 0, 0, 0)
-HELD = (0, 2, 3, 4)
-BY_PASS = (0, 1, 2)
+RUN = 4
+WORDS = PASSES * (C + N)
+
+HEAD = 2 * C
+TILES_BEFORE_WEIGHTS = (4, 7)
+VECTOR_EXPERT = 1
+TAIL = E - 2
 
 
 def tile_moe_pre_lin_gelu_kernel(tc, xT, w, b, gate, offs, out):
@@ -40,151 +38,125 @@ def tile_moe_pre_lin_gelu_kernel(tc, xT, w, b, gate, offs, out):
         psum = ctx.enter_context(tc.psum_pool(name="psum", bufs=8))
 
         offsets = keep.tile([P, S // LIST_ROW], U16, name="offsets")
-        nc.sync.dma_start(offsets[:], offs)
-        gate_all = keep.tile([P, S], F32, name="gate_all")
-        nc.sync.dma_start(gate_all[:], gate[0:P, :])
+        gate_rows = keep.tile([P, S], F32, name="gate_rows")
         bias = keep.tile([P, ROW_TILES, E], F32, name="bias")
-
+        token_tiles = [(g, t) for g in range(PASSES) for t in range(PACK)]
+        x_raw = {(g, t): keep.tile([P, T], F32, name="x_raw_%d_%d" % (g, t)) for g, t in token_tiles}
+        w_raw = [keep.tile([P, PASSES, PACK, N], F32, name="w_raw_%d" % e) for e in range(E)]
         x_rows = xT.rearrange("(g p t) c -> g t p c", p=P, t=PACK)
-        w_rows = w.rearrange("e (g p j) n -> e g p j n", p=P, j=PACK)
-        x_raw = {}
-        w_raw = {}
-        x_pieces = [(g, t) for g in range(PASSES) for t in range(PACK)]
-        w_pieces = [(e, g) for e in range(E) for g in range(PASSES)]
-        nx = 0
-        nw = 0
-        for i, kind in enumerate(LOADS):
-            if kind == "x":
-                g, t = x_pieces[nx]
-                nx = nx + 1
-                x_raw[g, t] = keep.tile([P, T], F32, name="x_raw_%d_%d" % (g, t))
-                nc.sync.dma_start(x_raw[g, t][:], x_rows[g, t])
-            else:
-                e, g = w_pieces[nw]
-                nw = nw + 1
-                if g == 0:
-                    w_raw[e] = keep.tile([P, PASSES, PACK, N], F32, name="w_raw_%d" % e)
+        w_rows = w.rearrange("e (g p t) n -> e g p t n", p=P, t=PACK)
+
+        for i, (g, t) in enumerate(token_tiles):
+            if i in TILES_BEFORE_WEIGHTS:
+                w_pass = TILES_BEFORE_WEIGHTS.index(i)
+                nc.sync.dma_start(w_raw[0][:, w_pass], w_rows[0, w_pass])
+            nc.sync.dma_start(x_raw[g, t][:], x_rows[g, t])
+            if i == 0:
+                nc.sync.dma_start(offsets[:], offs)
+                nc.sync.dma_start(gate_rows[:, 0:HEAD], gate[0:P, 0:HEAD])
+                nc.sync.dma_start(gate_rows[:, HEAD:S], gate[0:P, HEAD:S])
+        for e in range(1, E):
+            for g in range(PASSES):
                 nc.sync.dma_start(w_raw[e][:, g], w_rows[e, g])
-            if i == 6:
+            if e == 1:
                 nc.sync.dma_start(bias[:], b.rearrange("(r p) e -> p r e", p=P))
 
-        zeros = keep.tile([P, C], F32, name="zeros")
+        zeros = keep.tile([P, (E - TAIL) * C], F32, name="zeros")
         nc.gpsimd.memset(zeros[:], 0.0)
         warm = keep.tile([P, 1], F32, name="warm")
         nc.scalar.activation(warm[:], zeros[:, 0:1], GELU)
 
-        windows = []
+        out_tiles = [keep.tile([P, T], F32, name="out_tile_%d" % r) for r in range(ROW_TILES)]
         for r in range(ROW_TILES):
-            windows.append(keep.tile([P, T], F32, name="window_%d" % r))
-            (nc.gpsimd if r == 2 else nc.vector).memset(windows[r][:], 0.0)
-        y_own = [keep.tile([P, max(1, E - MERGE_FROM) * C], F32, name="y_%d" % r) for r in range(ROW_TILES)]
-        x_codes = {}
-        x_scales = {}
-        w_codes = {}
-        w_scales = {}
-        gathered = [keep.tile([P, PACK, S], F32, name="gathered_%d" % g) for g in range(PASSES)]
+            (nc.gpsimd if r == ROW_TILES - 1 else nc.vector).memset(out_tiles[r][:], 0.0)
 
-        def gather(g, t, lo, hi):
-            src = x_raw[g, t][:].indirect(offsets[:, lo // LIST_ROW : hi // LIST_ROW])
-            nc.vector.tensor_tensor(gathered[g][:, t, lo:hi], src, gate_all[:, lo:hi], MULT)
+        gated = [keep.tile([P, PACK, S], F32, name="gated_%d" % g) for g in range(PASSES)]
+        rounded = [keep.tile([P, WORDS * PACK], BF16, name="rounded_%d" % e, align_bytes=64) for e in range(E)]
+        codes = [keep.tile([P, WORDS], U32, name="codes_%d" % e, align_bytes=64) for e in range(E)]
+        scales = [keep.tile([P, WORDS], U8, name="scales_%d" % e, align_bytes=64) for e in range(E)]
+        y_tail = [keep.tile([P, (E - TAIL) * C], F32, name="y_tail_%d" % r) for r in range(ROW_TILES)]
+        w_words = {}
 
-        UNIT = PASSES * (C + N)
-        rounded = [keep.tile([P, UNIT * PACK], BF16, name="rounded_%d" % e, align_bytes=64) for e in range(E)]
-        codes = [keep.tile([P, UNIT], U32, name="codes_%d" % e, align_bytes=64) for e in range(E)]
-        scales = [keep.tile([P, UNIT], U8, name="scales_%d" % e, align_bytes=64) for e in range(E)]
+        def listed(tile, lo, hi):
+            return tile[:].indirect(offsets[:, lo // LIST_ROW : hi // LIST_ROW])
 
-        def quantize(e, lo, hi):
-            nc.vector.quantize_mx(
-                out=codes[e][:, lo:hi].bitcast(FP8X4),
-                scales=scales[e][:, lo:hi],
-                in_=rounded[e][:, lo * PACK : hi * PACK],
-            )
-
-        def round_x(g, e):
+        def round_slots(g, e):
             nc.scalar.copy(
-                rounded[e][:, g * C * PACK : (g + 1) * C * PACK].rearrange("p (c i j) -> p c j i", i=4, j=PACK),
-                gathered[g][:, :, e * C : (e + 1) * C].rearrange("p j (c i) -> p c j i", i=4),
+                rounded[e][:, g * C * PACK : (g + 1) * C * PACK].rearrange("p (c i t) -> p c t i", i=RUN, t=PACK),
+                gated[g][:, :, e * C : (e + 1) * C].rearrange("p t (c i) -> p c t i", i=RUN),
             )
-            x_codes[e, g] = codes[e][:, g * C : (g + 1) * C]
-            x_scales[e, g] = scales[e][:, g * C : (g + 1) * C]
 
-        def quantize_w(e, r):
-            if e < BY_ROWS and r > 0:
-                return
-            lo, n = (0, N) if e < BY_ROWS else (r * P, P)
-            base = PASSES * (C + lo)
-            dst = rounded[e][:, base * PACK : (base + PASSES * n) * PACK].rearrange(
-                "p (g c i j) -> p g c j i", g=PASSES, i=4, j=PACK
+        def quantize_expert(e, lo, width):
+            first = PASSES * (C + lo)
+            last = first + PASSES * width
+            dst = rounded[e][:, first * PACK : last * PACK].rearrange(
+                "p (g c i t) -> p g c t i", g=PASSES, i=RUN, t=PACK
             )
-            src = w_raw[e][:, :, :, lo : lo + n].rearrange("p g j (c i) -> p g c j i", i=4)
-            cut = V_COLS[e] * n // N // 4
-            if cut > 0:
-                nc.vector.tensor_copy(dst[:, :, 0:cut], src[:, :, 0:cut])
-            if cut < n // 4 and e in BY_PASS:
+            src = w_raw[e][:, :, :, lo : lo + width].rearrange("p g t (c i) -> p g c t i", i=RUN)
+            if e == VECTOR_EXPERT:
+                nc.vector.tensor_copy(dst, src)
+            elif e < TAIL:
                 for g in range(PASSES):
-                    nc.scalar.copy(dst[:, g, cut : n // 4], src[:, g, cut : n // 4])
-            elif cut < n // 4:
-                nc.scalar.copy(dst[:, :, cut : n // 4], src[:, :, cut : n // 4])
-            quantize(e, base if lo > 0 else 0, base + PASSES * n)
-            for rr in range(lo // P, (lo + n) // P):
+                    nc.scalar.copy(dst[:, g], src[:, g])
+            else:
+                nc.scalar.copy(dst, src)
+            words = slice(first if lo > 0 else 0, last)
+            nc.vector.quantize_mx(
+                out=codes[e][:, words].bitcast(FP8X4),
+                scales=scales[e][:, words],
+                in_=rounded[e][:, words.start * PACK : words.stop * PACK],
+            )
+            for col in range(lo, lo + width, P):
                 for g in range(PASSES):
-                    at = base + g * n + rr * P - lo
-                    w_codes[e, rr, g] = codes[e][:, at : at + P]
-                    w_scales[e, rr, g] = scales[e][:, at : at + P]
+                    w_words[e, col // P, g] = first + g * width + col - lo
 
         def y_place(e, r):
-            if e in HELD and e < MERGE_FROM and e + YLEAD < E:
-                return w_raw[e + YLEAD][:, 1, r, N - P : N]
-            if e < MERGE_FROM:
-                return gathered[0][:, r, e * C : (e + 1) * C]
-            return y_own[r][:, (e - MERGE_FROM) * C : (e - MERGE_FROM + 1) * C]
-
-        def scatter(r, lo, hi, src):
-            window = windows[r][:].indirect(offsets[:, lo // LIST_ROW : hi // LIST_ROW])
-            if hi - lo >= T // 8:
-                nc.vector.tensor_copy(window, src)
-            else:
-                nc.vector.tensor_tensor(window, src, zeros[:, 0 : hi - lo], ADD)
+            if e >= TAIL:
+                return y_tail[r][:, (e - TAIL) * C : (e - TAIL + 1) * C]
+            if e == 0:
+                return gated[0][:, r, 0:C]
+            return w_raw[e + 1][:, PASSES - 1, r, N - C : N]
 
         def product(e, r):
             acc = psum.tile([P, C], F32, name="acc")
             for g in range(PASSES):
+                w_cols = slice(w_words[e, r, g], w_words[e, r, g] + P)
+                x_cols = slice(g * C, (g + 1) * C)
                 nc.tensor.matmul_mx(
                     out=acc[:],
-                    lhsT=w_codes[e, r, g].bitcast(FP8X4),
-                    lhsT_scale=w_scales[e, r, g],
-                    rhs=x_codes[e, g].bitcast(FP8X4),
-                    rhs_scale=x_scales[e, g],
+                    lhsT=codes[e][:, w_cols].bitcast(FP8X4),
+                    lhsT_scale=scales[e][:, w_cols],
+                    rhs=codes[e][:, x_cols].bitcast(FP8X4),
+                    rhs_scale=scales[e][:, x_cols],
                     start=(g == 0),
                     stop=(g == PASSES - 1),
                 )
             nc.scalar.activation(y_place(e, r), acc[:], GELU, bias=bias[:, r, e : e + 1])
 
-        for i, (g, t) in enumerate(x_pieces):
-            for lo, hi in XGROUPS if i >= SPLIT_FROM else ((0, S),):
-                gather(g, t, lo, hi)
+        def scatter(r, lo, hi, y):
+            nc.vector.tensor_tensor(listed(out_tiles[r], lo, hi), y, zeros[:, 0 : hi - lo], ADD)
+
+        for i, (g, t) in enumerate(token_tiles):
+            cut = i in (0, len(token_tiles) - 1)
+            for lo, hi in ((0, HEAD), (HEAD, S)) if cut else ((0, S),):
+                nc.vector.tensor_tensor(gated[g][:, t, lo:hi], listed(x_raw[g, t], lo, hi), gate_rows[:, lo:hi], MULT)
             if t == PACK - 1:
                 for e in range(E):
-                    round_x(g, e)
+                    round_slots(g, e)
 
-        for r in range(ROW_TILES):
-            quantize_w(0, r)
-        for e in range(MERGE_FROM):
-            for r in range(ROW_TILES):
-                if e + 1 < E:
-                    quantize_w(e + 1, r)
+        quantize_expert(0, 0, N)
+        for e in range(TAIL):
+            quantize_expert(e + 1, 0, N)
             for r in range(ROW_TILES):
                 product(e, r)
                 scatter(r, e * C, (e + 1) * C, y_place(e, r))
-                if e == E - 1:
-                    nc.sync.dma_start(out[r * P : (r + 1) * P, :], windows[r][:])
-        if MERGE_FROM < E:
-            for r in range(ROW_TILES + 1):
-                if r < ROW_TILES:
-                    for e in range(MERGE_FROM + 1, E):
-                        quantize_w(e, r)
-                if r > 0:
-                    for e in range(MERGE_FROM, E):
-                        product(e, r - 1)
-                    scatter(r - 1, MERGE_FROM * C, S, y_own[r - 1][:])
-                    nc.sync.dma_start(out[(r - 1) * P : r * P, :], windows[r - 1][:])
+
+        for step in range(ROW_TILES + 1):
+            if step < ROW_TILES:
+                quantize_expert(E - 1, step * P, P)
+            if step > 0:
+                r = step - 1
+                for e in range(TAIL, E):
+                    product(e, r)
+                scatter(r, TAIL * C, S, y_tail[r][:])
+                nc.sync.dma_start(out[r * P : (r + 1) * P, :], out_tiles[r][:])

from contextlib import ExitStack

import concourse.mybir as mybir

K, T, E, C, N = 1024, 1280, 6, 128, 384
S = E * C
FLOPS = 2 * K * N * S
BYTES = 4 * (K * T + E * K * N + N * E + S + N * T) + 2 * S

F32 = mybir.dt.float32
BF16 = mybir.dt.bfloat16
U32 = mybir.dt.uint32
U16 = mybir.dt.uint16
U8 = mybir.dt.uint8
FP8X4 = mybir.dt.float8_e4m3fn_x4
GELU = mybir.ActivationFunctionType.Gelu_apprx_tanh
ADD = mybir.AluOpType.add
MULT = mybir.AluOpType.mult

P = 128
PACK = 4
PASSES = K // (P * PACK)
ROW_TILES = N // P
LIST_ROW = 16
RUN = 4
WORDS = PASSES * (C + N)

HEAD = 2 * C
TILES_BEFORE_WEIGHTS = (4, 7)
VECTOR_EXPERT = 1
TAIL = E - 2


def tile_moe_pre_lin_gelu_kernel(tc, xT, w, b, gate, offs, out):
    nc = tc.nc
    with ExitStack() as ctx:
        keep = ctx.enter_context(tc.tile_pool(name="keep", bufs=1))
        psum = ctx.enter_context(tc.psum_pool(name="psum", bufs=8))

        offsets = keep.tile([P, S // LIST_ROW], U16, name="offsets")
        gate_rows = keep.tile([P, S], F32, name="gate_rows")
        bias = keep.tile([P, ROW_TILES, E], F32, name="bias")
        token_tiles = [(g, t) for g in range(PASSES) for t in range(PACK)]
        x_raw = {(g, t): keep.tile([P, T], F32, name="x_raw_%d_%d" % (g, t)) for g, t in token_tiles}
        w_raw = [keep.tile([P, PASSES, PACK, N], F32, name="w_raw_%d" % e) for e in range(E)]
        x_rows = xT.rearrange("(g p t) c -> g t p c", p=P, t=PACK)
        w_rows = w.rearrange("e (g p t) n -> e g p t n", p=P, t=PACK)

        for i, (g, t) in enumerate(token_tiles):
            if i in TILES_BEFORE_WEIGHTS:
                w_pass = TILES_BEFORE_WEIGHTS.index(i)
                nc.sync.dma_start(w_raw[0][:, w_pass], w_rows[0, w_pass])
            nc.sync.dma_start(x_raw[g, t][:], x_rows[g, t])
            if i == 0:
                nc.sync.dma_start(offsets[:], offs)
                nc.sync.dma_start(gate_rows[:, 0:HEAD], gate[0:P, 0:HEAD])
                nc.sync.dma_start(gate_rows[:, HEAD:S], gate[0:P, HEAD:S])
        for e in range(1, E):
            for g in range(PASSES):
                nc.sync.dma_start(w_raw[e][:, g], w_rows[e, g])
            if e == 1:
                nc.sync.dma_start(bias[:], b.rearrange("(r p) e -> p r e", p=P))

        zeros = keep.tile([P, (E - TAIL) * C], F32, name="zeros")
        nc.gpsimd.memset(zeros[:], 0.0)
        warm = keep.tile([P, 1], F32, name="warm")
        nc.scalar.activation(warm[:], zeros[:, 0:1], GELU)

        out_tiles = [keep.tile([P, T], F32, name="out_tile_%d" % r) for r in range(ROW_TILES)]
        for r in range(ROW_TILES):
            (nc.gpsimd if r == ROW_TILES - 1 else nc.vector).memset(out_tiles[r][:], 0.0)

        gated = [keep.tile([P, PACK, S], F32, name="gated_%d" % g) for g in range(PASSES)]
        rounded = [keep.tile([P, WORDS * PACK], BF16, name="rounded_%d" % e, align_bytes=64) for e in range(E)]
        codes = [keep.tile([P, WORDS], U32, name="codes_%d" % e, align_bytes=64) for e in range(E)]
        scales = [keep.tile([P, WORDS], U8, name="scales_%d" % e, align_bytes=64) for e in range(E)]
        y_tail = [keep.tile([P, (E - TAIL) * C], F32, name="y_tail_%d" % r) for r in range(ROW_TILES)]
        w_words = {}

        def listed(tile, lo, hi):
            return tile[:].indirect(offsets[:, lo // LIST_ROW : hi // LIST_ROW])

        def round_slots(g, e):
            nc.scalar.copy(
                rounded[e][:, g * C * PACK : (g + 1) * C * PACK].rearrange("p (c i t) -> p c t i", i=RUN, t=PACK),
                gated[g][:, :, e * C : (e + 1) * C].rearrange("p t (c i) -> p c t i", i=RUN),
            )

        def quantize_expert(e, lo, width):
            first = PASSES * (C + lo)
            last = first + PASSES * width
            dst = rounded[e][:, first * PACK : last * PACK].rearrange(
                "p (g c i t) -> p g c t i", g=PASSES, i=RUN, t=PACK
            )
            src = w_raw[e][:, :, :, lo : lo + width].rearrange("p g t (c i) -> p g c t i", i=RUN)
            if e == VECTOR_EXPERT:
                nc.vector.tensor_copy(dst, src)
            elif e < TAIL:
                for g in range(PASSES):
                    nc.scalar.copy(dst[:, g], src[:, g])
            else:
                nc.scalar.copy(dst, src)
            words = slice(first if lo > 0 else 0, last)
            nc.vector.quantize_mx(
                out=codes[e][:, words].bitcast(FP8X4),
                scales=scales[e][:, words],
                in_=rounded[e][:, words.start * PACK : words.stop * PACK],
            )
            for col in range(lo, lo + width, P):
                for g in range(PASSES):
                    w_words[e, col // P, g] = first + g * width + col - lo

        def y_place(e, r):
            if e >= TAIL:
                return y_tail[r][:, (e - TAIL) * C : (e - TAIL + 1) * C]
            if e == 0:
                return gated[0][:, r, 0:C]
            return w_raw[e + 1][:, PASSES - 1, r, N - C : N]

        def product(e, r):
            acc = psum.tile([P, C], F32, name="acc")
            for g in range(PASSES):
                w_cols = slice(w_words[e, r, g], w_words[e, r, g] + P)
                x_cols = slice(g * C, (g + 1) * C)
                nc.tensor.matmul_mx(
                    out=acc[:],
                    lhsT=codes[e][:, w_cols].bitcast(FP8X4),
                    lhsT_scale=scales[e][:, w_cols],
                    rhs=codes[e][:, x_cols].bitcast(FP8X4),
                    rhs_scale=scales[e][:, x_cols],
                    start=(g == 0),
                    stop=(g == PASSES - 1),
                )
            nc.scalar.activation(y_place(e, r), acc[:], GELU, bias=bias[:, r, e : e + 1])

        def scatter(r, lo, hi, y):
            nc.vector.tensor_tensor(listed(out_tiles[r], lo, hi), y, zeros[:, 0 : hi - lo], ADD)

        for i, (g, t) in enumerate(token_tiles):
            cut = i in (0, len(token_tiles) - 1)
            for lo, hi in ((0, HEAD), (HEAD, S)) if cut else ((0, S),):
                nc.vector.tensor_tensor(gated[g][:, t, lo:hi], listed(x_raw[g, t], lo, hi), gate_rows[:, lo:hi], MULT)
            if t == PACK - 1:
                for e in range(E):
                    round_slots(g, e)

        quantize_expert(0, 0, N)
        for e in range(TAIL):
            quantize_expert(e + 1, 0, N)
            for r in range(ROW_TILES):
                product(e, r)
                scatter(r, e * C, (e + 1) * C, y_place(e, r))

        for step in range(ROW_TILES + 1):
            if step < ROW_TILES:
                quantize_expert(E - 1, step * P, P)
            if step > 0:
                r = step - 1
                for e in range(TAIL, E):
                    product(e, r)
                scatter(r, TAIL * C, S, y_tail[r][:])
                nc.sync.dma_start(out[r * P : (r + 1) * P, :], out_tiles[r][:])
